import numpy as np
import ml_dtypes


def mxq(x, axis, fmt="e4m3"):
    dtype, down = {"e4m3": (ml_dtypes.float8_e4m3fn, 7), "e5m2": (ml_dtypes.float8_e5m2, 14)}[fmt]
    v = np.moveaxis(np.asarray(x, np.float32).astype(ml_dtypes.bfloat16).astype(np.float64), axis, -1)
    blocks = v.reshape(v.shape[:-1] + (-1, 32))
    amax = np.abs(blocks).max(-1, keepdims=True)
    byte = np.maximum(np.where(amax > 0, np.frexp(amax)[1] - 1 + 127, 0) - down, 1)
    scale = np.exp2(byte - 127.0)
    codes = (blocks / scale).astype(np.float32).astype(dtype).astype(np.float64)
    return np.moveaxis((codes * scale).reshape(v.shape), -1, axis)


WIDE = False


def mx_kscale(k):
    if not WIDE:
        return np.ones(k)
    levels = np.array([30, -30])
    if k % 512:
        return np.exp2(np.random.permutation(np.resize(levels, k // 32))).repeat(32)
    a = np.empty((k // 512, 16))
    for p in range(k // 512):
        a[p, :8] = np.random.permutation(np.resize(levels, 8))
        for g in range(8):
            far = levels[np.abs(levels - a[p, g]) >= 10]
            a[p, g + 8] = far[np.random.randint(len(far))]
    return np.exp2(a.ravel()).repeat(32)


BF16 = ml_dtypes.bfloat16


def bf(x):
    return np.asarray(x, np.float32).astype(BF16)


def f64(x):
    return np.asarray(x).astype(np.float64)


E2M1 = np.array([0.0, 0.5, 1.0, 1.5, 2.0, 3.0, 4.0, 6.0, -0.0, -0.5, -1.0, -1.5, -2.0, -3.0, -4.0, -6.0])


def pack_weight(w, fmt):
    k, n = w.shape
    w = f64(bf(w)).reshape(k // 32, 32, n)
    amax = np.abs(w).max(1)
    if fmt in ("e4m3", "e5m2"):
        byte = np.frexp(amax)[1] - 1 + 127 - (7 if fmt == "e4m3" else 14)
    else:
        mant, ex = np.frexp(amax / 6.0)
        byte = np.where(mant > 0.5, ex, ex - 1) + 127
    byte = np.clip(np.where(amax > 0, byte, 1), 1, 254)
    scaled = (w * np.exp2(127.0 - byte)[:, None, :]).reshape(k, n).astype(np.float32)
    by_word = np.ascontiguousarray(scaled.reshape(k // 512, 128, 4, n).transpose(0, 1, 3, 2))
    if fmt in ("e4m3", "e5m2"):
        words = by_word.astype(ml_dtypes.float8_e4m3fn if fmt == "e4m3" else ml_dtypes.float8_e5m2).view(np.uint8)
    else:
        c = by_word.astype(ml_dtypes.float4_e2m1fn).view(np.uint8) & 0xF
        words = c[..., 0::2] | (c[..., 1::2] << 4)
    return np.ascontiguousarray(words), np.ascontiguousarray(byte.astype(np.uint8).reshape(k // 512, 16, n))


def unpack_weight(words, scales, fmt):
    g, p, n, _ = words.shape
    if fmt in ("e4m3", "e5m2"):
        vals = np.ascontiguousarray(words).view(ml_dtypes.float8_e4m3fn if fmt == "e4m3" else ml_dtypes.float8_e5m2).astype(np.float64)
    else:
        nib = np.empty((g, p, n, 4), np.uint8)
        nib[..., 0::2] = words & 0xF
        nib[..., 1::2] = words >> 4
        vals = E2M1[nib]
    vals = vals * np.repeat(np.exp2(scales.astype(np.float64) - 127.0), 8, axis=1)[..., None]
    return vals.transpose(0, 1, 3, 2).reshape(g * 512, n)

def planes(Y):
    n, m = Y.shape
    b = f64(bf(Y)).reshape(n // 32, 32, m)
    amax = np.abs(b).max(1)
    byte = np.clip(np.where(amax > 0, np.frexp(amax)[1] - 1 + 127 - 7, 1), 1, 254)
    codes = (b * np.exp2(127.0 - byte)[:, None, :]).reshape(n, m).astype(np.float32).astype(ml_dtypes.float8_e4m3fn).view(np.uint8)
    words = codes.reshape(n // 512, 128, 4, m).transpose(0, 1, 3, 2)
    return np.ascontiguousarray(words), np.ascontiguousarray(byte.astype(np.uint8).reshape(n // 512, 16, m))


T, K, N = 1536, 2048, 1024
LEAK, GAIN = 0.8, 0.6

def setup_inputs():
    s = mx_kscale(K)
    amp = np.exp(0.8 * np.random.randn(N))
    E = np.random.randn(K, T) * np.exp(np.random.randn(K, T) - 1.0)
    slope_words, slope_scales = pack_weight(E * s[:, None], "e5m2")
    recon = np.random.randn(K, N) / np.sqrt(K) * amp[None, :]
    return {
        "slope_words": slope_words,
        "slope_scales": slope_scales,
        "recon": bf(recon / s[:, None]),
        "mode_ref": bf(0.4 * np.random.randn(N) * amp),
        "gain": bf(GAIN * (1.0 + 0.15 * np.random.randn(N))),
        "leak": bf(LEAK * (1.0 + 0.04 * np.random.randn(N))),
        "prev": bf(np.random.randn(T, N) * amp[None, :]),
    }

def reference(slope_words, slope_scales, recon, mode_ref, gain, leak, prev):
    E = unpack_weight(slope_words, slope_scales, "e5m2")
    R = mxq(f64(recon), 0, "e4m3")
    modes = E.T @ R
    err = modes - f64(mode_ref)
    y = f64(leak) * f64(prev) - f64(gain) * err
    Y = y.T
    words, scales = planes(Y)
    return y, words, scales

@@ -1,0 +1,257 @@
+from contextlib import ExitStack
+
+import concourse.mybir as mybir
+from concourse.masks import make_identity
+
+T, K, N = 1536, 2048, 1024
+FLOPS = 2 * T * K * N
+
+F32 = mybir.dt.float32
+BF16 = mybir.dt.bfloat16
+I32 = mybir.dt.int32
+U32 = mybir.dt.uint32
+U8 = mybir.dt.uint8
+E4M3X4 = mybir.dt.float8_e4m3fn_x4
+E5M2X4 = mybir.dt.float8_e5m2_x4
+IDENTITY = mybir.ActivationFunctionType.Identity
+MULT = mybir.AluOpType.mult
+ADD = mybir.AluOpType.add
+
+P = 128
+PACK = 4
+GROUP = P * PACK
+PASSES = K // GROUP
+HALVES = N // GROUP
+BLOCKS = T // GROUP
+UNITS = HALVES * BLOCKS
+
+
+def tile_leaky_modal_integrator_k2_kernel(
+    tc, slope_words, slope_scales, recon, mode_ref, gain, leak, prev, out_0, out_1, out_2
+):
+    nc = tc.nc
+    with ExitStack() as ctx:
+        sb = ctx.enter_context(tc.tile_pool(name="sb", bufs=1))
+        ps = ctx.enter_context(tc.psum_pool(name="ps", bufs=1))
+        ctx.enter_context(tc.manual_schedule())
+
+        def sbuf(name, shape, dtype):
+            return sb.tile(shape, dtype, name=name, align_bytes=64)
+
+        mx_bank = [ps.tile([P, GROUP], F32, name="mx%d" % t) for t in range(PACK)]
+        tr_bank = [ps.tile([P, GROUP], F32, name="tr%d" % j) for j in range(PACK)]
+
+        ident = sbuf("ident", [P, P], F32)
+        e_words = {(g, b): sbuf("ew%d%d" % (g, b), [P, GROUP], U32) for g in range(PASSES) for b in range(BLOCKS)}
+        e_scales = [sbuf("es%d" % b, [P, PASSES * GROUP], U8) for b in range(BLOCKS)]
+        r_raw = {(h, g): sbuf("rr%d%d" % (h, g), [P, PACK, GROUP], BF16) for h in range(HALVES) for g in range(PASSES)}
+        r_sorted = {(g, s): sbuf("rs%d%d" % (g, s), [P, 2 * GROUP], BF16) for g in range(2) for s in range(2)}
+        r_codes = {
+            (h, g, s): sbuf("rc%d%d%d" % (h, g, s), [P, 2 * P], U32)
+            for h in range(HALVES) for g in range(PASSES) for s in range(2)
+        }
+        r_scales = {
+            (h, g, s): sbuf("rq%d%d%d" % (h, g, s), [P, 2 * P], U8)
+            for h in range(HALVES) for g in range(PASSES) for s in range(2)
+        }
+        prev_rows = [sbuf("prev%d" % k, [P, PACK, GROUP], BF16) for k in range(UNITS)]
+        ref_bf = sbuf("ref_bf", [P, HALVES, PACK], BF16)
+        gain_bf = sbuf("gain_bf", [P, HALVES, PACK], BF16)
+        leak_bf = sbuf("leak_bf", [P, HALVES, PACK], BF16)
+        leak_f = sbuf("leak_f", [P, HALVES, PACK], F32)
+        neg_gain = sbuf("neg_gain", [P, HALVES, PACK], F32)
+        gain_ref = sbuf("gain_ref", [P, HALVES, PACK], F32)
+        held = [sbuf("held%d" % i, [P, PACK, GROUP], F32) for i in range(2)]
+        y_modes = [sbuf("ym%d" % i, [P, PACK, GROUP], F32) for i in range(2)]
+        y_bf = [sbuf("yb%d" % i, [P, PACK * GROUP], BF16) for i in range(2)]
+        y_rows = [sbuf("yr%d" % k, [P, PACK, GROUP], F32) for k in range(UNITS)]
+        y_codes = [sbuf("yc%d" % k, [P, GROUP], U32) for k in range(UNITS)]
+        y_scales = sbuf("ysc", [P, T], U8)
+
+        def span(i, width=GROUP):
+            return slice(i * width, (i + 1) * width)
+
+        def load_recon(h, g):
+            src = recon[span(g), span(h)].rearrange("(p j) c -> p j c", j=PACK)
+            nc.sync.dma_start(out=r_raw[h, g][:], in_=src)
+
+        def load_words(g, b):
+            src = slope_words[g].rearrange("p n t -> p (n t)")[:, span(b, PACK * GROUP)]
+            nc.sync.dma_start(out=e_words[g, b][:].bitcast(I32), in_=src.bitcast(I32))
+
+        def load_scales(b):
+            for q in range(4):
+                src = slope_scales[:, 4 * q : 4 * q + 4, span(b)].bitcast(I32).rearrange("g r w -> r g w")
+                dst = e_scales[b][32 * q : 32 * q + 4, :].bitcast(I32).rearrange("r (g w) -> r g w", g=PASSES)
+                nc.sync.dma_start(out=dst, in_=src)
+
+        def load_prev(k):
+            h, b = divmod(k, BLOCKS)
+            src = prev[span(b), span(h)].rearrange("(j p) c -> p j c", p=P)
+            nc.sync.dma_start(out=prev_rows[k][:], in_=src)
+
+        def sort_recon(h, g, s):
+            dst = r_sorted[g % 2, s][:].rearrange("p (t mm i j) -> p mm t i j", t=2, i=2, j=PACK)
+            src = r_raw[h, g][:].rearrange("p j (mm i t) -> p mm t i j", i=2, t=PACK)[:, :, 2 * s : 2 * s + 2, :, :]
+            if s == h:
+                nc.vector.tensor_copy(out=dst, in_=src)
+            elif (h, g) == (0, 0):
+                for t in range(2):
+                    nc.scalar.activation(out=dst[:, :, t, :, :], in_=src[:, :, t, :, :], func=IDENTITY)
+            else:
+                nc.scalar.copy(out=dst, in_=src)
+
+        def quantize_recon(h, g, s):
+            nc.vector.quantize_mx(
+                out=r_codes[h, g, s][:].bitcast(E4M3X4), scales=r_scales[h, g, s][:], in_=r_sorted[g % 2, s][:]
+            )
+
+        def mx_pass(k, t, g):
+            h, b = divmod(k, BLOCKS)
+            s, cols = t // 2, span(t % 2, P)
+            nc.tensor.matmul_mx(
+                out=mx_bank[t][:],
+                lhsT=r_codes[h, g, s][:, cols].bitcast(E4M3X4),
+                lhsT_scale=r_scales[h, g, s][:, cols],
+                rhs=e_words[g, b][:].bitcast(E5M2X4),
+                rhs_scale=e_scales[b][:, span(g)],
+                start=(g == 0),
+                stop=(g == PASSES - 1),
+            )
+
+        def turn_prev(k):
+            for u in range(2):
+                for j in range(PACK):
+                    words = prev_rows[k][:, j, :].bitcast(F32)
+                    nc.tensor.transpose(tr_bank[(2 * k + u) % 4][:, span(j, P)], words[:, u : 2 * P : 2], ident[:])
+
+        def hold_term(k, t):
+            h = k // BLOCKS
+            pairs = tr_bank[(2 * k + t // 2) % 4][:].bitcast(BF16)
+            nc.scalar.activation(
+                out=held[k % 2][:, t, :], in_=pairs[:, t % 2 : 2 * GROUP : 2], func=IDENTITY,
+                scale=leak_f[:, h, t : t + 1], bias=gain_ref[:, h, t : t + 1],
+            )
+
+        def update(k, t, cols):
+            h = k // BLOCKS
+            nc.vector.scalar_tensor_tensor(
+                out=y_modes[k % 2][:, t, cols], in0=mx_bank[t][:, cols], scalar=neg_gain[:, h, t : t + 1],
+                in1=held[k % 2][:, t, cols], op0=MULT, op1=ADD,
+            )
+
+        def turn_y(k, j, t):
+            nc.tensor.transpose(tr_bank[(2 * k + j) % 4][:, span(t, P)], y_modes[k % 2][:, t, span(j, P)], ident[:])
+
+        def copy_y(k, j):
+            nc.scalar.copy(
+                out=y_rows[k][:, j, :].rearrange("p (m t) -> p m t", t=PACK),
+                in_=tr_bank[(2 * k + j) % 4][:].rearrange("p (t m) -> p m t", t=PACK),
+            )
+
+        def round_y(k):
+            nc.vector.tensor_copy(
+                out=y_bf[k % 2][:].rearrange("p (c t) -> p c t", t=PACK),
+                in_=y_modes[k % 2][:].rearrange("p t c -> p c t"),
+            )
+
+        def quantize_y(k):
+            h, b = divmod(k, BLOCKS)
+            nc.vector.quantize_mx(
+                out=y_codes[k][:].bitcast(E4M3X4), scales=y_scales[4 * h : P, span(b)], in_=y_bf[k % 2][:]
+            )
+
+        def store_y(k, tiles):
+            h, b = divmod(k, BLOCKS)
+            dst = out_0[span(b), span(h)].rearrange("(j p) c -> p j c", p=P)
+            nc.sync.dma_start(out=dst[:, tiles, :], in_=y_rows[k][:, tiles, :])
+
+        def store_codes(k):
+            h, b = divmod(k, BLOCKS)
+            dst = out_1[h].rearrange("p n t -> p (n t)")[:, span(b, PACK * GROUP)]
+            nc.sync.dma_start(out=dst.bitcast(I32), in_=y_codes[k][:].bitcast(I32))
+
+        make_identity(nc, ident[:])
+        for b in range(BLOCKS):
+            nc.vector.memset(e_scales[b][:].bitcast(U32), 0)
+
+        load_recon(0, 0)
+        load_recon(0, 1)
+        load_scales(0)
+        load_words(0, 0)
+        load_recon(0, 2)
+        load_words(1, 0)
+        load_prev(0)
+        for vec, dst in ((leak, leak_bf), (gain, gain_bf), (mode_ref, ref_bf)):
+            nc.sync.dma_start(out=dst[:], in_=vec.rearrange("(h p t) -> p h t", p=P, t=PACK))
+        load_recon(0, 3)
+        load_words(2, 0)
+        load_words(3, 0)
+        for b in (1, 2):
+            load_scales(b)
+            for g in range(PASSES):
+                load_words(g, b)
+            load_prev(b)
+            load_recon(1, 2 * b - 2)
+            load_recon(1, 2 * b - 1)
+        for k in range(BLOCKS, UNITS):
+            load_prev(k)
+
+        for g in range(PASSES):
+            if g == PASSES - 1:
+                nc.vector.tensor_copy(out=leak_f[:], in_=leak_bf[:])
+                nc.vector.tensor_scalar(out=neg_gain[:], in0=gain_bf[:], scalar1=-1.0, scalar2=None, op0=MULT)
+                nc.vector.tensor_tensor(out=gain_ref[:], in0=gain_bf[:], in1=ref_bf[:], op=MULT)
+            sort_recon(0, g, 0)
+            sort_recon(0, g, 1)
+            if g > 0:
+                quantize_recon(0, g - 1, 1)
+            quantize_recon(0, g, 0)
+        quantize_recon(0, PASSES - 1, 1)
+
+        for k in range(UNITS):
+            last = k == UNITS - 1
+            first = range(PACK) if k == 0 else (0, 1)
+            for g in range(2 if k == 0 else PASSES):
+                for t in first:
+                    mx_pass(k, t, g)
+            turn_prev(k)
+            for t in range(PACK):
+                hold_term(k, t)
+            if k == 0:
+                for g in (2, 3):
+                    for t in range(PACK):
+                        mx_pass(k, t, g)
+            else:
+                for t in (2, 3):
+                    for g in range(PASSES):
+                        mx_pass(k, t, g)
+            for t in range(PACK - 1):
+                update(k, t, span(0))
+            if last:
+                for j in range(PACK):
+                    update(k, PACK - 1, span(j, P))
+            else:
+                update(k, PACK - 1, span(0))
+            for t in range(PACK):
+                for j in range(PACK):
+                    turn_y(k, j, t)
+            late = (2 * k - 2, 2 * k - 1) if k in (1, 2) else ()
+            for g in late:
+                sort_recon(1, g, 0)
+                sort_recon(1, g, 1)
+            for s in range(2):
+                for g in late:
+                    quantize_recon(1, g, s)
+            round_y(k)
+            for j in range(PACK):
+                copy_y(k, j)
+                store_y(k, slice(j, j + 1))
+                if j == 1:
+                    quantize_y(k)
+                if j == 2:
+                    store_codes(k)
+        for q in range(4):
+            nc.scalar.dma_start(
+                out=out_2[:, 4 * q : 4 * q + 4, :].bitcast(I32), in_=y_scales[32 * q : 32 * q + 8, :].bitcast(I32)
+            )

@@ -44,16 +44,10 @@ def tile_leaky_modal_integrator_k2_kernel(
         ident = sbuf("ident", [P, P], F32)
         e_words = {(g, b): sbuf("ew%d%d" % (g, b), [P, GROUP], U32) for g in range(PASSES) for b in range(BLOCKS)}
         e_scales = [sbuf("es%d" % b, [P, PASSES * GROUP], U8) for b in range(BLOCKS)]
-        r_raw = {(h, g): sbuf("rr%d%d" % (h, g), [P, PACK, GROUP], BF16) for h in range(HALVES) for g in range(PASSES)}
+        r_raw = [sbuf("rr%d" % g, [P, PACK, GROUP], BF16) for g in range(PASSES)]
         r_sorted = {(g, s): sbuf("rs%d%d" % (g, s), [P, 2 * GROUP], BF16) for g in range(2) for s in range(2)}
-        r_codes = {
-            (h, g, s): sbuf("rc%d%d%d" % (h, g, s), [P, 2 * P], U32)
-            for h in range(HALVES) for g in range(PASSES) for s in range(2)
-        }
-        r_scales = {
-            (h, g, s): sbuf("rq%d%d%d" % (h, g, s), [P, 2 * P], U8)
-            for h in range(HALVES) for g in range(PASSES) for s in range(2)
-        }
+        r_codes = {(h, g): sbuf("rc%d%d" % (h, g), [P, GROUP], U32) for h in range(HALVES) for g in range(PASSES)}
+        r_scales = {(h, g): sbuf("rq%d%d" % (h, g), [P, GROUP], U8) for h in range(HALVES) for g in range(PASSES)}
         prev_rows = [sbuf("prev%d" % k, [P, PACK, GROUP], BF16) for k in range(UNITS)]
         ref_bf = sbuf("ref_bf", [P, HALVES, PACK], BF16)
         gain_bf = sbuf("gain_bf", [P, HALVES, PACK], BF16)
@@ -67,13 +61,19 @@ def tile_leaky_modal_integrator_k2_kernel(
         y_rows = [sbuf("yr%d" % k, [P, PACK, GROUP], F32) for k in range(UNITS)]
         y_codes = [sbuf("yc%d" % k, [P, GROUP], U32) for k in range(UNITS)]
         y_scales = sbuf("ysc", [P, T], U8)
+        leak_row = sbuf("leak_row", [P, GROUP], F32)
+        neg_gain_row = sbuf("neg_gain_row", [P, GROUP], F32)
+        gain_ref_row = sbuf("gain_ref_row", [P, GROUP], F32)
+        held_rows = sbuf("held_rows", [P, PACK, GROUP], F32)
+        scaled = [sbuf("scaled%d" % i, [P, GROUP], F32) for i in range(2)]
+        y_pairs = [sbuf("yp%d" % j, [P, GROUP], BF16) for j in range(PACK)]
 
         def span(i, width=GROUP):
             return slice(i * width, (i + 1) * width)
 
         def load_recon(h, g):
             src = recon[span(g), span(h)].rearrange("(p j) c -> p j c", j=PACK)
-            nc.sync.dma_start(out=r_raw[h, g][:], in_=src)
+            nc.sync.dma_start(out=r_raw[g][:], in_=src)
 
         def load_words(g, b):
             src = slope_words[g].rearrange("p n t -> p (n t)")[:, span(b, PACK * GROUP)]
@@ -92,8 +92,8 @@ def tile_leaky_modal_integrator_k2_kernel(
 
         def sort_recon(h, g, s):
             dst = r_sorted[g % 2, s][:].rearrange("p (t mm i j) -> p mm t i j", t=2, i=2, j=PACK)
-            src = r_raw[h, g][:].rearrange("p j (mm i t) -> p mm t i j", i=2, t=PACK)[:, :, 2 * s : 2 * s + 2, :, :]
-            if s == h:
+            src = r_raw[g][:].rearrange("p j (mm i t) -> p mm t i j", i=2, t=PACK)[:, :, 2 * s : 2 * s + 2, :, :]
+            if s == 0:
                 nc.vector.tensor_copy(out=dst, in_=src)
             elif (h, g) == (0, 0):
                 for t in range(2):
@@ -102,17 +102,17 @@ def tile_leaky_modal_integrator_k2_kernel(
                 nc.scalar.copy(out=dst, in_=src)
 
         def quantize_recon(h, g, s):
+            cols = span(s, 2 * P)
             nc.vector.quantize_mx(
-                out=r_codes[h, g, s][:].bitcast(E4M3X4), scales=r_scales[h, g, s][:], in_=r_sorted[g % 2, s][:]
+                out=r_codes[h, g][:, cols].bitcast(E4M3X4), scales=r_scales[h, g][:, cols], in_=r_sorted[g % 2, s][:]
             )
 
         def mx_pass(k, t, g):
             h, b = divmod(k, BLOCKS)
-            s, cols = t // 2, span(t % 2, P)
             nc.tensor.matmul_mx(
                 out=mx_bank[t][:],
-                lhsT=r_codes[h, g, s][:, cols].bitcast(E4M3X4),
-                lhsT_scale=r_scales[h, g, s][:, cols],
+                lhsT=r_codes[h, g][:, span(t, P)].bitcast(E4M3X4),
+                lhsT_scale=r_scales[h, g][:, span(t, P)],
                 rhs=e_words[g, b][:].bitcast(E5M2X4),
                 rhs_scale=e_scales[b][:, span(g)],
                 start=(g == 0),
@@ -133,11 +133,11 @@ def tile_leaky_modal_integrator_k2_kernel(
                 scale=leak_f[:, h, t : t + 1], bias=gain_ref[:, h, t : t + 1],
             )
 
-        def update(k, t, cols):
+        def update(k, t):
             h = k // BLOCKS
             nc.vector.scalar_tensor_tensor(
-                out=y_modes[k % 2][:, t, cols], in0=mx_bank[t][:, cols], scalar=neg_gain[:, h, t : t + 1],
-                in1=held[k % 2][:, t, cols], op0=MULT, op1=ADD,
+                out=y_modes[k % 2][:, t, :], in0=mx_bank[t][:], scalar=neg_gain[:, h, t : t + 1],
+                in1=held[k % 2][:, t, :], op0=MULT, op1=ADD,
             )
 
         def turn_y(k, j, t):
@@ -150,15 +150,22 @@ def tile_leaky_modal_integrator_k2_kernel(
             )
 
         def round_y(k):
-            nc.vector.tensor_copy(
-                out=y_bf[k % 2][:].rearrange("p (c t) -> p c t", t=PACK),
-                in_=y_modes[k % 2][:].rearrange("p t c -> p c t"),
-            )
+            dst = y_bf[k % 2][:].rearrange("p (c i t) -> p c t i", i=2, t=PACK)
+            src = y_modes[k % 2][:].rearrange("p t (c i) -> p c t i", i=2)
+            if k >= UNITS - 3:
+                split = P if k == UNITS - 3 else 168
+                nc.vector.tensor_copy(out=dst[:, 0:split, :, :], in_=src[:, 0:split, :, :])
+                nc.scalar.copy(out=dst[:, split : 2 * P, :, :], in_=src[:, split : 2 * P, :, :])
+            else:
+                nc.vector.tensor_copy(out=dst, in_=src)
 
-        def quantize_y(k):
+        def quantize_y(k, first=0, count=PACK):
             h, b = divmod(k, BLOCKS)
+            lo, hi = first * P, (first + count) * P
             nc.vector.quantize_mx(
-                out=y_codes[k][:].bitcast(E4M3X4), scales=y_scales[4 * h : P, span(b)], in_=y_bf[k % 2][:]
+                out=y_codes[k][:, lo:hi].bitcast(E4M3X4),
+                scales=y_scales[4 * h : P, b * GROUP + lo : b * GROUP + hi],
+                in_=y_bf[k % 2][:, PACK * lo : PACK * hi],
             )
 
         def store_y(k, tiles):
@@ -166,10 +173,85 @@ def tile_leaky_modal_integrator_k2_kernel(
             dst = out_0[span(b), span(h)].rearrange("(j p) c -> p j c", p=P)
             nc.sync.dma_start(out=dst[:, tiles, :], in_=y_rows[k][:, tiles, :])
 
-        def store_codes(k):
+        def store_codes(k, first=0, count=PACK):
             h, b = divmod(k, BLOCKS)
-            dst = out_1[h].rearrange("p n t -> p (n t)")[:, span(b, PACK * GROUP)]
-            nc.sync.dma_start(out=dst.bitcast(I32), in_=y_codes[k][:].bitcast(I32))
+            lo, hi = first * P, (first + count) * P
+            dst = out_1[h].rearrange("p n t -> p (n t)")[:, PACK * (b * GROUP + lo) : PACK * (b * GROUP + hi)]
+            nc.sync.dma_start(out=dst.bitcast(I32), in_=y_codes[k][:, lo:hi].bitcast(I32))
+
+        last = UNITS - 1
+
+        def spread(row, columns, bank):
+            for t in range(PACK):
+                nc.tensor.transpose(bank[:, span(t, P)], columns[:, 1, t : t + 1].to_broadcast([P, P]), ident[:])
+            nc.scalar.copy(
+                out=row[:].rearrange("p (m t) -> p m t", t=PACK), in_=bank[:].rearrange("p (t m) -> p m t", t=PACK)
+            )
+
+        def leak_rows(j):
+            nc.vector.tensor_tensor(out=held_rows[:, j, :], in0=prev_rows[last][:, j, :], in1=leak_row[:], op=MULT)
+
+        def hold_rows(j):
+            nc.vector.tensor_tensor(out=held_rows[:, j, :], in0=held_rows[:, j, :], in1=gain_ref_row[:], op=ADD)
+
+        def mx_rows(j):
+            for g in range(PASSES):
+                nc.tensor.matmul_mx(
+                    out=mx_bank[j][:],
+                    lhsT=e_words[g, BLOCKS - 1][:, span(j, P)].bitcast(E5M2X4),
+                    lhsT_scale=e_scales[BLOCKS - 1][:, span(PACK * g + j, P)],
+                    rhs=r_codes[1, g][:].bitcast(E4M3X4),
+                    rhs_scale=r_scales[1, g][:],
+                    start=(g == 0),
+                    stop=(g == PASSES - 1),
+                )
+
+        def scale_rows(j):
+            for half in range(2):
+                ms = span(half, P // 2)
+                nc.vector.tensor_tensor(
+                    out=scaled[j % 2][:].rearrange("p (m t) -> p m t", t=PACK)[:, ms, :],
+                    in0=mx_bank[j][:].rearrange("p (t m) -> p m t", t=PACK)[:, ms, :],
+                    in1=neg_gain_row[:].rearrange("p (m t) -> p m t", t=PACK)[:, ms, :],
+                    op=MULT,
+                )
+
+        def add_rows(j):
+            for half in range(2):
+                cols = span(half, 2 * P)
+                nc.vector.tensor_tensor(
+                    out=y_rows[last][:, j, cols], in0=scaled[j % 2][:, cols], in1=held_rows[:, j, cols], op=ADD
+                )
+
+        def by_pair(ap):
+            return ap.rearrange("p (m u e) -> p u m e", u=2, e=2)
+
+        def round_rows(j):
+            nc.scalar.copy(
+                out=y_pairs[j][:].rearrange("p (u m e) -> p u m e", u=2, e=2), in_=by_pair(y_rows[last][:, j, :])
+            )
+
+        def add_rows_rounded(j):
+            for u in range(2):
+                nc.vector.tensor_tensor(
+                    out=y_pairs[j][:].rearrange("p (u m e) -> p u m e", u=2, e=2)[:, u, :, :],
+                    in0=by_pair(scaled[j % 2][:])[:, u, :, :],
+                    in1=by_pair(held_rows[:, j, :])[:, u, :, :],
+                    op=ADD,
+                )
+
+        def turn_pairs(bank, first, count):
+            for j in range(count):
+                for u in range(2):
+                    words = y_pairs[first + j][:].bitcast(F32)
+                    nc.tensor.transpose(bank[:, span(2 * j + u, P)], words[:, span(u, P)], ident[:])
+
+        def copy_pairs(bank, first, count):
+            words = y_bf[last % 2][:].bitcast(F32)[:, 2 * P * first : 2 * P * (first + count)]
+            nc.scalar.copy(
+                out=words.rearrange("p (j r u) -> p j r u", j=count, u=2),
+                in_=bank[:, 0 : 2 * P * count].rearrange("p (j u r) -> p j r u", j=count, u=2),
+            )
 
         make_identity(nc, ident[:])
         for b in range(BLOCKS):
@@ -180,28 +262,32 @@ def tile_leaky_modal_integrator_k2_kernel(
         load_scales(0)
         load_words(0, 0)
         load_recon(0, 2)
-        load_words(1, 0)
-        load_prev(0)
         for vec, dst in ((leak, leak_bf), (gain, gain_bf), (mode_ref, ref_bf)):
             nc.sync.dma_start(out=dst[:], in_=vec.rearrange("(h p t) -> p h t", p=P, t=PACK))
+        load_words(1, 0)
+        load_prev(0)
         load_recon(0, 3)
         load_words(2, 0)
         load_words(3, 0)
-        for b in (1, 2):
-            load_scales(b)
-            for g in range(PASSES):
-                load_words(g, b)
-            load_prev(b)
-            load_recon(1, 2 * b - 2)
-            load_recon(1, 2 * b - 1)
-        for k in range(BLOCKS, UNITS):
-            load_prev(k)
+        load_prev(1)
+        load_scales(1)
+        for g in range(PASSES):
+            load_words(g, 1)
 
         for g in range(PASSES):
-            if g == PASSES - 1:
+            if g == 2:
                 nc.vector.tensor_copy(out=leak_f[:], in_=leak_bf[:])
                 nc.vector.tensor_scalar(out=neg_gain[:], in0=gain_bf[:], scalar1=-1.0, scalar2=None, op0=MULT)
                 nc.vector.tensor_tensor(out=gain_ref[:], in0=gain_bf[:], in1=ref_bf[:], op=MULT)
+            if g == 3:
+                for t in range(PACK):
+                    mx_pass(0, t, 0)
+                spread(leak_row, leak_f, tr_bank[1])
+                spread(neg_gain_row, neg_gain, tr_bank[2])
+                spread(gain_ref_row, gain_ref, tr_bank[3])
+                for t in range(PACK):
+                    mx_pass(0, t, 1)
+                turn_prev(0)
             sort_recon(0, g, 0)
             sort_recon(0, g, 1)
             if g > 0:
@@ -209,49 +295,109 @@ def tile_leaky_modal_integrator_k2_kernel(
             quantize_recon(0, g, 0)
         quantize_recon(0, PASSES - 1, 1)
 
-        for k in range(UNITS):
-            last = k == UNITS - 1
-            first = range(PACK) if k == 0 else (0, 1)
-            for g in range(2 if k == 0 else PASSES):
-                for t in first:
-                    mx_pass(k, t, g)
-            turn_prev(k)
+        load_recon(1, 0)
+        load_prev(2)
+        load_recon(1, 1)
+        load_scales(2)
+        for g in range(PASSES):
+            load_words(g, 2)
+        load_recon(1, 2)
+        load_recon(1, 3)
+        for k in (3, last, 4):
+            load_prev(k)
+
+        for t in range(PACK):
+            hold_term(0, t)
+        for g in (2, 3):
+            for t in range(PACK):
+                mx_pass(0, t, g)
+        for t in range(PACK):
+            update(0, t)
+        turn_prev(1)
+
+        def sort_late(g, s):
+            if 0 <= g < PASSES:
+                sort_recon(1, g, s)
+
+        def quantize_late(g, s):
+            if 0 <= g < PASSES:
+                quantize_recon(1, g, s)
+
+        for k in range(1, last):
+            early, late = 2 * k - 3, 2 * k - 2
             for t in range(PACK):
                 hold_term(k, t)
-            if k == 0:
-                for g in (2, 3):
-                    for t in range(PACK):
-                        mx_pass(k, t, g)
-            else:
-                for t in (2, 3):
-                    for g in range(PASSES):
-                        mx_pass(k, t, g)
-            for t in range(PACK - 1):
-                update(k, t, span(0))
-            if last:
-                for j in range(PACK):
-                    update(k, PACK - 1, span(j, P))
-            else:
-                update(k, PACK - 1, span(0))
-            for t in range(PACK):
-                for j in range(PACK):
-                    turn_y(k, j, t)
-            late = (2 * k - 2, 2 * k - 1) if k in (1, 2) else ()
-            for g in late:
-                sort_recon(1, g, 0)
-                sort_recon(1, g, 1)
-            for s in range(2):
-                for g in late:
-                    quantize_recon(1, g, s)
-            round_y(k)
+            sort_late(early, 0)
+            sort_late(early, 1)
+            if k == 4:
+                leak_rows(2)
+            quantize_late(early - 1, 1)
+            quantize_late(early, 0)
+            round_y(k - 1)
+            if k == 4:
+                hold_rows(2)
+                leak_rows(3)
+            for g in range(PASSES):
+                for t in (0, 1):
+                    mx_pass(k, t, g)
+            sort_late(late, 0)
+            quantize_y(k - 1)
+            quantize_late(late - 1, 1)
+            update(k, 0)
+            quantize_late(late, 0)
+            update(k, 1)
+            rows = (0, 1) if k == 3 else ()
+            for j in rows:
+                leak_rows(j)
+            if k == 4:
+                hold_rows(3)
             for j in range(PACK):
-                copy_y(k, j)
-                store_y(k, slice(j, j + 1))
-                if j == 1:
-                    quantize_y(k)
-                if j == 2:
-                    store_codes(k)
+                for t in range(PACK):
+                    turn_y(k - 1, j, t)
+                copy_y(k - 1, j)
+                store_y(k - 1, slice(j, j + 1))
+            store_codes(k - 1)
+            sort_late(late, 1)
+            for t in (2, 3):
+                for g in range(PASSES):
+                    mx_pass(k, t, g)
+                update(k, t)
+                if t == 2:
+                    for j in rows:
+                        hold_rows(j)
+            if k + 1 < last:
+                turn_prev(k + 1)
+
+        k = last - 1
+        for t in range(PACK):
+            for j in range(PACK):
+                turn_y(k, j, t)
+        round_y(k)
+        quantize_y(k)
+        for j in range(PACK):
+            copy_y(k, j)
+            store_y(k, slice(j, j + 1))
+        store_codes(k)
+        for j in range(PACK - 1):
+            mx_rows(j)
+            scale_rows(j)
+            add_rows(j)
+            round_rows(j)
+            store_y(last, slice(j, j + 1))
+        mx_rows(3)
+        scale_rows(3)
+        add_rows_rounded(3)
+        add_rows(3)
+        parts = ((0, 2), (2, 1), (3, 1))
+        for i, (first, count) in enumerate(parts):
+            turn_pairs(tr_bank[i], first, count)
+            copy_pairs(tr_bank[i], first, count)
+            quantize_y(last, first, count)
+        store_y(last, slice(3, 4))
+        store_codes(last, 0, 2)
+        store_codes(last, 2, 2)
         for q in range(4):
-            nc.scalar.dma_start(
+            queue = nc.scalar if q < 3 else nc.sync
+            queue.dma_start(
                 out=out_2[:, 4 * q : 4 * q + 4, :].bitcast(I32), in_=y_scales[32 * q : 32 * q + 8, :].bitcast(I32)
             )

@@ -16,6 +16,7 @@ E5M2X4 = mybir.dt.float8_e5m2_x4
 IDENTITY = mybir.ActivationFunctionType.Identity
 MULT = mybir.AluOpType.mult
 ADD = mybir.AluOpType.add
+SUBTRACT = mybir.AluOpType.subtract
 
 P = 128
 PACK = 4
@@ -24,6 +25,7 @@ PASSES = K // GROUP
 HALVES = N // GROUP
 BLOCKS = T // GROUP
 UNITS = HALVES * BLOCKS
+VECTOR_PAIRS = (192, 256, 160, 0, 104)
 
 
 def tile_leaky_modal_integrator_k2_kernel(
@@ -36,22 +38,23 @@ def tile_leaky_modal_integrator_k2_kernel(
         ctx.enter_context(tc.manual_schedule())
 
         def sbuf(name, shape, dtype):
-            return sb.tile(shape, dtype, name=name, align_bytes=64)
+            return sb.tile(shape, dtype, name=name, align_bytes=256 if dtype in (U32, U8) else 64)
 
         mx_bank = [ps.tile([P, GROUP], F32, name="mx%d" % t) for t in range(PACK)]
         tr_bank = [ps.tile([P, GROUP], F32, name="tr%d" % j) for j in range(PACK)]
 
         ident = sbuf("ident", [P, P], F32)
-        e_words = {(g, b): sbuf("ew%d%d" % (g, b), [P, GROUP], U32) for g in range(PASSES) for b in range(BLOCKS)}
+        e_first = [sbuf("ew%d" % g, [P, GROUP], U32) for g in range(PASSES)]
+        e_pairs = {(i, b): sbuf("ew%d%d" % (i, b), [P, 2, GROUP], U32) for i in range(2) for b in (1, 2)}
         e_scales = [sbuf("es%d" % b, [P, PASSES * GROUP], U8) for b in range(BLOCKS)]
         r_raw = [sbuf("rr%d" % g, [P, PACK, GROUP], BF16) for g in range(PASSES)]
         r_sorted = {(g, s): sbuf("rs%d%d" % (g, s), [P, 2 * GROUP], BF16) for g in range(2) for s in range(2)}
         r_codes = {(h, g): sbuf("rc%d%d" % (h, g), [P, GROUP], U32) for h in range(HALVES) for g in range(PASSES)}
         r_scales = {(h, g): sbuf("rq%d%d" % (h, g), [P, GROUP], U8) for h in range(HALVES) for g in range(PASSES)}
         prev_rows = [sbuf("prev%d" % k, [P, PACK, GROUP], BF16) for k in range(UNITS)]
-        ref_bf = sbuf("ref_bf", [P, HALVES, PACK], BF16)
-        gain_bf = sbuf("gain_bf", [P, HALVES, PACK], BF16)
-        leak_bf = sbuf("leak_bf", [P, HALVES, PACK], BF16)
+        vec_raw = sbuf("vec_raw", [P, GROUP], BF16)
+        vec_cols = sbuf("vec_cols", [P, 3, HALVES, PACK], BF16)
+        leak_bf, gain_bf, ref_bf = (vec_cols[:, i, :, :] for i in range(3))
         leak_f = sbuf("leak_f", [P, HALVES, PACK], F32)
         neg_gain = sbuf("neg_gain", [P, HALVES, PACK], F32)
         gain_ref = sbuf("gain_ref", [P, HALVES, PACK], F32)
@@ -61,8 +64,7 @@ def tile_leaky_modal_integrator_k2_kernel(
         y_rows = [sbuf("yr%d" % k, [P, PACK, GROUP], F32) for k in range(UNITS)]
         y_codes = [sbuf("yc%d" % k, [P, GROUP], U32) for k in range(UNITS)]
         y_scales = sbuf("ysc", [P, T], U8)
-        leak_row = sbuf("leak_row", [P, GROUP], F32)
-        neg_gain_row = sbuf("neg_gain_row", [P, GROUP], F32)
+        vec_rows = sbuf("vec_rows", [P, 3, GROUP], BF16)
         gain_ref_row = sbuf("gain_ref_row", [P, GROUP], F32)
         held_rows = sbuf("held_rows", [P, PACK, GROUP], F32)
         scaled = [sbuf("scaled%d" % i, [P, GROUP], F32) for i in range(2)]
@@ -75,9 +77,16 @@ def tile_leaky_modal_integrator_k2_kernel(
             src = recon[span(g), span(h)].rearrange("(p j) c -> p j c", j=PACK)
             nc.sync.dma_start(out=r_raw[g][:], in_=src)
 
-        def load_words(g, b):
-            src = slope_words[g].rearrange("p n t -> p (n t)")[:, span(b, PACK * GROUP)]
-            nc.sync.dma_start(out=e_words[g, b][:].bitcast(I32), in_=src.bitcast(I32))
+        def load_first_words(g):
+            src = slope_words[g].rearrange("p n t -> p (n t)")[:, span(0, PACK * GROUP)]
+            nc.sync.dma_start(out=e_first[g][:].bitcast(I32), in_=src.bitcast(I32))
+
+        def load_word_pair(i, b):
+            src = slope_words[2 * i : 2 * i + 2].rearrange("g p n t -> p g (n t)")[:, :, span(b, PACK * GROUP)]
+            nc.sync.dma_start(out=e_pairs[i, b][:].bitcast(I32), in_=src.bitcast(I32))
+
+        def e_words(g, b):
+            return e_first[g][:] if b == 0 else e_pairs[g // 2, b][:, g % 2, :]
 
         def load_scales(b):
             for q in range(4):
@@ -113,7 +122,7 @@ def tile_leaky_modal_integrator_k2_kernel(
                 out=mx_bank[t][:],
                 lhsT=r_codes[h, g][:, span(t, P)].bitcast(E4M3X4),
                 lhsT_scale=r_scales[h, g][:, span(t, P)],
-                rhs=e_words[g, b][:].bitcast(E5M2X4),
+                rhs=e_words(g, b).bitcast(E5M2X4),
                 rhs_scale=e_scales[b][:, span(g)],
                 start=(g == 0),
                 stop=(g == PASSES - 1),
@@ -152,12 +161,11 @@ def tile_leaky_modal_integrator_k2_kernel(
         def round_y(k):
             dst = y_bf[k % 2][:].rearrange("p (c i t) -> p c t i", i=2, t=PACK)
             src = y_modes[k % 2][:].rearrange("p t (c i) -> p c t i", i=2)
-            if k >= UNITS - 3:
-                split = P if k == UNITS - 3 else 168
+            split = VECTOR_PAIRS[k]
+            if split > 0:
                 nc.vector.tensor_copy(out=dst[:, 0:split, :, :], in_=src[:, 0:split, :, :])
+            if split < 2 * P:
                 nc.scalar.copy(out=dst[:, split : 2 * P, :, :], in_=src[:, split : 2 * P, :, :])
-            else:
-                nc.vector.tensor_copy(out=dst, in_=src)
 
         def quantize_y(k, first=0, count=PACK):
             h, b = divmod(k, BLOCKS)
@@ -181,15 +189,17 @@ def tile_leaky_modal_integrator_k2_kernel(
 
         last = UNITS - 1
 
-        def spread(row, columns, bank):
-            for t in range(PACK):
-                nc.tensor.transpose(bank[:, span(t, P)], columns[:, 1, t : t + 1].to_broadcast([P, P]), ident[:])
+        def spread(i):
+            words = vec_cols[:, i, 1, :].bitcast(F32)
+            for u in range(2):
+                nc.tensor.transpose(tr_bank[i][:, span(u, P)], words[:, u : u + 1].to_broadcast([P, P]), ident[:])
             nc.scalar.copy(
-                out=row[:].rearrange("p (m t) -> p m t", t=PACK), in_=bank[:].rearrange("p (t m) -> p m t", t=PACK)
+                out=vec_rows[:, i, :].bitcast(F32).rearrange("p (m u) -> p m u", u=2),
+                in_=tr_bank[i][:, 0 : 2 * P].rearrange("p (u m) -> p m u", u=2),
             )
 
         def leak_rows(j):
-            nc.vector.tensor_tensor(out=held_rows[:, j, :], in0=prev_rows[last][:, j, :], in1=leak_row[:], op=MULT)
+            nc.vector.tensor_tensor(out=held_rows[:, j, :], in0=prev_rows[last][:, j, :], in1=vec_rows[:, 0, :], op=MULT)
 
         def hold_rows(j):
             nc.vector.tensor_tensor(out=held_rows[:, j, :], in0=held_rows[:, j, :], in1=gain_ref_row[:], op=ADD)
@@ -198,7 +208,7 @@ def tile_leaky_modal_integrator_k2_kernel(
             for g in range(PASSES):
                 nc.tensor.matmul_mx(
                     out=mx_bank[j][:],
-                    lhsT=e_words[g, BLOCKS - 1][:, span(j, P)].bitcast(E5M2X4),
+                    lhsT=e_words(g, BLOCKS - 1)[:, span(j, P)].bitcast(E5M2X4),
                     lhsT_scale=e_scales[BLOCKS - 1][:, span(PACK * g + j, P)],
                     rhs=r_codes[1, g][:].bitcast(E4M3X4),
                     rhs_scale=r_scales[1, g][:],
@@ -212,7 +222,7 @@ def tile_leaky_modal_integrator_k2_kernel(
                 nc.vector.tensor_tensor(
                     out=scaled[j % 2][:].rearrange("p (m t) -> p m t", t=PACK)[:, ms, :],
                     in0=mx_bank[j][:].rearrange("p (t m) -> p m t", t=PACK)[:, ms, :],
-                    in1=neg_gain_row[:].rearrange("p (m t) -> p m t", t=PACK)[:, ms, :],
+                    in1=vec_rows[:, 1, :].rearrange("p (m t) -> p m t", t=PACK)[:, ms, :],
                     op=MULT,
                 )
 
@@ -220,7 +230,7 @@ def tile_leaky_modal_integrator_k2_kernel(
             for half in range(2):
                 cols = span(half, 2 * P)
                 nc.vector.tensor_tensor(
-                    out=y_rows[last][:, j, cols], in0=scaled[j % 2][:, cols], in1=held_rows[:, j, cols], op=ADD
+                    out=y_rows[last][:, j, cols], in0=held_rows[:, j, cols], in1=scaled[j % 2][:, cols], op=SUBTRACT
                 )
 
         def by_pair(ap):
@@ -235,9 +245,9 @@ def tile_leaky_modal_integrator_k2_kernel(
             for u in range(2):
                 nc.vector.tensor_tensor(
                     out=y_pairs[j][:].rearrange("p (u m e) -> p u m e", u=2, e=2)[:, u, :, :],
-                    in0=by_pair(scaled[j % 2][:])[:, u, :, :],
-                    in1=by_pair(held_rows[:, j, :])[:, u, :, :],
-                    op=ADD,
+                    in0=by_pair(held_rows[:, j, :])[:, u, :, :],
+                    in1=by_pair(scaled[j % 2][:])[:, u, :, :],
+                    op=SUBTRACT,
                 )
 
         def turn_pairs(bank, first, count):
@@ -254,40 +264,43 @@ def tile_leaky_modal_integrator_k2_kernel(
             )
 
         make_identity(nc, ident[:])
+        nc.vector.memset(vec_raw[:].bitcast(U32), 0)
         for b in range(BLOCKS):
             nc.vector.memset(e_scales[b][:].bitcast(U32), 0)
 
         load_recon(0, 0)
+        for i, vec in enumerate((leak, gain, mode_ref)):
+            nc.scalar.dma_start(out=vec_raw[2 * i : 2 * i + 2, :], in_=vec.rearrange("(h c) -> h c", h=HALVES))
         load_recon(0, 1)
         load_scales(0)
-        load_words(0, 0)
+        load_first_words(0)
         load_recon(0, 2)
-        for vec, dst in ((leak, leak_bf), (gain, gain_bf), (mode_ref, ref_bf)):
-            nc.sync.dma_start(out=dst[:], in_=vec.rearrange("(h p t) -> p h t", p=P, t=PACK))
-        load_words(1, 0)
+        load_first_words(1)
         load_prev(0)
         load_recon(0, 3)
-        load_words(2, 0)
-        load_words(3, 0)
+        load_first_words(2)
+        load_first_words(3)
         load_prev(1)
         load_scales(1)
-        for g in range(PASSES):
-            load_words(g, 1)
+        load_word_pair(0, 1)
+        load_word_pair(1, 1)
 
         for g in range(PASSES):
+            if g == 1:
+                for u in range(2):
+                    nc.tensor.transpose(tr_bank[3][:, span(u, P)], vec_raw[:].bitcast(F32)[:, u : 2 * P : 2], ident[:])
+                nc.vector.tensor_copy(
+                    out=vec_cols[:].bitcast(F32).rearrange("p i h u -> p (i h) u"),
+                    in_=tr_bank[3][:, 0 : 2 * P].rearrange("p (u r) -> p r u", u=2)[:, 0 : 3 * HALVES, :],
+                )
             if g == 2:
-                nc.vector.tensor_copy(out=leak_f[:], in_=leak_bf[:])
-                nc.vector.tensor_scalar(out=neg_gain[:], in0=gain_bf[:], scalar1=-1.0, scalar2=None, op0=MULT)
-                nc.vector.tensor_tensor(out=gain_ref[:], in0=gain_bf[:], in1=ref_bf[:], op=MULT)
+                for i in range(3):
+                    spread(i)
+                nc.vector.tensor_copy(out=leak_f[:], in_=leak_bf)
+                nc.vector.tensor_scalar(out=neg_gain[:], in0=gain_bf, scalar1=-1.0, scalar2=None, op0=MULT)
+                nc.vector.tensor_tensor(out=gain_ref[:], in0=gain_bf, in1=ref_bf, op=MULT)
             if g == 3:
-                for t in range(PACK):
-                    mx_pass(0, t, 0)
-                spread(leak_row, leak_f, tr_bank[1])
-                spread(neg_gain_row, neg_gain, tr_bank[2])
-                spread(gain_ref_row, gain_ref, tr_bank[3])
-                for t in range(PACK):
-                    mx_pass(0, t, 1)
-                turn_prev(0)
+                nc.vector.tensor_tensor(out=gain_ref_row[:], in0=vec_rows[:, 1, :], in1=vec_rows[:, 2, :], op=MULT)
             sort_recon(0, g, 0)
             sort_recon(0, g, 1)
             if g > 0:
@@ -299,16 +312,19 @@ def tile_leaky_modal_integrator_k2_kernel(
         load_prev(2)
         load_recon(1, 1)
         load_scales(2)
-        for g in range(PASSES):
-            load_words(g, 2)
+        load_word_pair(0, 2)
+        load_word_pair(1, 2)
+        load_prev(3)
         load_recon(1, 2)
         load_recon(1, 3)
-        for k in (3, last, 4):
-            load_prev(k)
+        load_prev(4)
+        load_prev(last)
 
-        for t in range(PACK):
-            hold_term(0, t)
-        for g in (2, 3):
+        for g in range(PASSES):
+            if g == 2:
+                turn_prev(0)
+                for t in range(PACK):
+                    hold_term(0, t)
             for t in range(PACK):
                 mx_pass(0, t, g)
         for t in range(PACK):
@@ -325,60 +341,60 @@ def tile_leaky_modal_integrator_k2_kernel(
 
         for k in range(1, last):
             early, late = 2 * k - 3, 2 * k - 2
+            rows = (2 * k - 6, 2 * k - 5) if k >= 3 else ()
             for t in range(PACK):
                 hold_term(k, t)
             sort_late(early, 0)
             sort_late(early, 1)
-            if k == 4:
-                leak_rows(2)
             quantize_late(early - 1, 1)
             quantize_late(early, 0)
             round_y(k - 1)
-            if k == 4:
-                hold_rows(2)
-                leak_rows(3)
+            for j in rows:
+                leak_rows(j)
             for g in range(PASSES):
                 for t in (0, 1):
                     mx_pass(k, t, g)
             sort_late(late, 0)
-            quantize_y(k - 1)
-            quantize_late(late - 1, 1)
+            if not rows:
+                quantize_y(k - 1)
             update(k, 0)
+            quantize_late(late - 1, 1)
             quantize_late(late, 0)
             update(k, 1)
-            rows = (0, 1) if k == 3 else ()
             for j in rows:
-                leak_rows(j)
-            if k == 4:
-                hold_rows(3)
+                hold_rows(j)
             for j in range(PACK):
                 for t in range(PACK):
                     turn_y(k - 1, j, t)
                 copy_y(k - 1, j)
                 store_y(k - 1, slice(j, j + 1))
-            store_codes(k - 1)
             sort_late(late, 1)
             for t in (2, 3):
                 for g in range(PASSES):
                     mx_pass(k, t, g)
                 update(k, t)
-                if t == 2:
-                    for j in rows:
-                        hold_rows(j)
+                if rows and t == 2:
+                    quantize_y(k - 1)
+            store_codes(k - 1)
             if k + 1 < last:
                 turn_prev(k + 1)
 
         k = last - 1
+        mx_rows(0)
         for t in range(PACK):
             for j in range(PACK):
                 turn_y(k, j, t)
+        scale_rows(0)
+        add_rows(0)
         round_y(k)
         quantize_y(k)
+        store_y(last, slice(0, 1))
         for j in range(PACK):
             copy_y(k, j)
             store_y(k, slice(j, j + 1))
         store_codes(k)
-        for j in range(PACK - 1):
+        round_rows(0)
+        for j in (1, 2):
             mx_rows(j)
             scale_rows(j)
             add_rows(j)

from contextlib import ExitStack

import concourse.mybir as mybir
from concourse.masks import make_identity

T, K, N = 1536, 2048, 1024
FLOPS = 2 * T * K * N

F32 = mybir.dt.float32
BF16 = mybir.dt.bfloat16
I32 = mybir.dt.int32
U32 = mybir.dt.uint32
U8 = mybir.dt.uint8
E4M3X4 = mybir.dt.float8_e4m3fn_x4
E5M2X4 = mybir.dt.float8_e5m2_x4
IDENTITY = mybir.ActivationFunctionType.Identity
MULT = mybir.AluOpType.mult
ADD = mybir.AluOpType.add
SUBTRACT = mybir.AluOpType.subtract

P = 128
PACK = 4
GROUP = P * PACK
PASSES = K // GROUP
HALVES = N // GROUP
BLOCKS = T // GROUP
UNITS = HALVES * BLOCKS
VECTOR_PAIRS = (192, 256, 160, 0, 104)


def tile_leaky_modal_integrator_k2_kernel(
    tc, slope_words, slope_scales, recon, mode_ref, gain, leak, prev, out_0, out_1, out_2
):
    nc = tc.nc
    with ExitStack() as ctx:
        sb = ctx.enter_context(tc.tile_pool(name="sb", bufs=1))
        ps = ctx.enter_context(tc.psum_pool(name="ps", bufs=1))
        ctx.enter_context(tc.manual_schedule())

        def sbuf(name, shape, dtype):
            return sb.tile(shape, dtype, name=name, align_bytes=256 if dtype in (U32, U8) else 64)

        mx_bank = [ps.tile([P, GROUP], F32, name="mx%d" % t) for t in range(PACK)]
        tr_bank = [ps.tile([P, GROUP], F32, name="tr%d" % j) for j in range(PACK)]

        ident = sbuf("ident", [P, P], F32)
        e_first = [sbuf("ew%d" % g, [P, GROUP], U32) for g in range(PASSES)]
        e_pairs = {(i, b): sbuf("ew%d%d" % (i, b), [P, 2, GROUP], U32) for i in range(2) for b in (1, 2)}
        e_scales = [sbuf("es%d" % b, [P, PASSES * GROUP], U8) for b in range(BLOCKS)]
        r_raw = [sbuf("rr%d" % g, [P, PACK, GROUP], BF16) for g in range(PASSES)]
        r_sorted = {(g, s): sbuf("rs%d%d" % (g, s), [P, 2 * GROUP], BF16) for g in range(2) for s in range(2)}
        r_codes = {(h, g): sbuf("rc%d%d" % (h, g), [P, GROUP], U32) for h in range(HALVES) for g in range(PASSES)}
        r_scales = {(h, g): sbuf("rq%d%d" % (h, g), [P, GROUP], U8) for h in range(HALVES) for g in range(PASSES)}
        prev_rows = [sbuf("prev%d" % k, [P, PACK, GROUP], BF16) for k in range(UNITS)]
        vec_raw = sbuf("vec_raw", [P, GROUP], BF16)
        vec_cols = sbuf("vec_cols", [P, 3, HALVES, PACK], BF16)
        leak_bf, gain_bf, ref_bf = (vec_cols[:, i, :, :] for i in range(3))
        leak_f = sbuf("leak_f", [P, HALVES, PACK], F32)
        neg_gain = sbuf("neg_gain", [P, HALVES, PACK], F32)
        gain_ref = sbuf("gain_ref", [P, HALVES, PACK], F32)
        held = [sbuf("held%d" % i, [P, PACK, GROUP], F32) for i in range(2)]
        y_modes = [sbuf("ym%d" % i, [P, PACK, GROUP], F32) for i in range(2)]
        y_bf = [sbuf("yb%d" % i, [P, PACK * GROUP], BF16) for i in range(2)]
        y_rows = [sbuf("yr%d" % k, [P, PACK, GROUP], F32) for k in range(UNITS)]
        y_codes = [sbuf("yc%d" % k, [P, GROUP], U32) for k in range(UNITS)]
        y_scales = sbuf("ysc", [P, T], U8)
        vec_rows = sbuf("vec_rows", [P, 3, GROUP], BF16)
        gain_ref_row = sbuf("gain_ref_row", [P, GROUP], F32)
        held_rows = sbuf("held_rows", [P, PACK, GROUP], F32)
        scaled = [sbuf("scaled%d" % i, [P, GROUP], F32) for i in range(2)]
        y_pairs = [sbuf("yp%d" % j, [P, GROUP], BF16) for j in range(PACK)]

        def span(i, width=GROUP):
            return slice(i * width, (i + 1) * width)

        def load_recon(h, g):
            src = recon[span(g), span(h)].rearrange("(p j) c -> p j c", j=PACK)
            nc.sync.dma_start(out=r_raw[g][:], in_=src)

        def load_first_words(g):
            src = slope_words[g].rearrange("p n t -> p (n t)")[:, span(0, PACK * GROUP)]
            nc.sync.dma_start(out=e_first[g][:].bitcast(I32), in_=src.bitcast(I32))

        def load_word_pair(i, b):
            src = slope_words[2 * i : 2 * i + 2].rearrange("g p n t -> p g (n t)")[:, :, span(b, PACK * GROUP)]
            nc.sync.dma_start(out=e_pairs[i, b][:].bitcast(I32), in_=src.bitcast(I32))

        def e_words(g, b):
            return e_first[g][:] if b == 0 else e_pairs[g // 2, b][:, g % 2, :]

        def load_scales(b):
            for q in range(4):
                src = slope_scales[:, 4 * q : 4 * q + 4, span(b)].bitcast(I32).rearrange("g r w -> r g w")
                dst = e_scales[b][32 * q : 32 * q + 4, :].bitcast(I32).rearrange("r (g w) -> r g w", g=PASSES)
                nc.sync.dma_start(out=dst, in_=src)

        def load_prev(k):
            h, b = divmod(k, BLOCKS)
            src = prev[span(b), span(h)].rearrange("(j p) c -> p j c", p=P)
            nc.sync.dma_start(out=prev_rows[k][:], in_=src)

        def sort_recon(h, g, s):
            dst = r_sorted[g % 2, s][:].rearrange("p (t mm i j) -> p mm t i j", t=2, i=2, j=PACK)
            src = r_raw[g][:].rearrange("p j (mm i t) -> p mm t i j", i=2, t=PACK)[:, :, 2 * s : 2 * s + 2, :, :]
            if s == 0:
                nc.vector.tensor_copy(out=dst, in_=src)
            elif (h, g) == (0, 0):
                for t in range(2):
                    nc.scalar.activation(out=dst[:, :, t, :, :], in_=src[:, :, t, :, :], func=IDENTITY)
            else:
                nc.scalar.copy(out=dst, in_=src)

        def quantize_recon(h, g, s):
            cols = span(s, 2 * P)
            nc.vector.quantize_mx(
                out=r_codes[h, g][:, cols].bitcast(E4M3X4), scales=r_scales[h, g][:, cols], in_=r_sorted[g % 2, s][:]
            )

        def mx_pass(k, t, g):
            h, b = divmod(k, BLOCKS)
            nc.tensor.matmul_mx(
                out=mx_bank[t][:],
                lhsT=r_codes[h, g][:, span(t, P)].bitcast(E4M3X4),
                lhsT_scale=r_scales[h, g][:, span(t, P)],
                rhs=e_words(g, b).bitcast(E5M2X4),
                rhs_scale=e_scales[b][:, span(g)],
                start=(g == 0),
                stop=(g == PASSES - 1),
            )

        def turn_prev(k):
            for u in range(2):
                for j in range(PACK):
                    words = prev_rows[k][:, j, :].bitcast(F32)
                    nc.tensor.transpose(tr_bank[(2 * k + u) % 4][:, span(j, P)], words[:, u : 2 * P : 2], ident[:])

        def hold_term(k, t):
            h = k // BLOCKS
            pairs = tr_bank[(2 * k + t // 2) % 4][:].bitcast(BF16)
            nc.scalar.activation(
                out=held[k % 2][:, t, :], in_=pairs[:, t % 2 : 2 * GROUP : 2], func=IDENTITY,
                scale=leak_f[:, h, t : t + 1], bias=gain_ref[:, h, t : t + 1],
            )

        def update(k, t):
            h = k // BLOCKS
            nc.vector.scalar_tensor_tensor(
                out=y_modes[k % 2][:, t, :], in0=mx_bank[t][:], scalar=neg_gain[:, h, t : t + 1],
                in1=held[k % 2][:, t, :], op0=MULT, op1=ADD,
            )

        def turn_y(k, j, t):
            nc.tensor.transpose(tr_bank[(2 * k + j) % 4][:, span(t, P)], y_modes[k % 2][:, t, span(j, P)], ident[:])

        def copy_y(k, j):
            nc.scalar.copy(
                out=y_rows[k][:, j, :].rearrange("p (m t) -> p m t", t=PACK),
                in_=tr_bank[(2 * k + j) % 4][:].rearrange("p (t m) -> p m t", t=PACK),
            )

        def round_y(k):
            dst = y_bf[k % 2][:].rearrange("p (c i t) -> p c t i", i=2, t=PACK)
            src = y_modes[k % 2][:].rearrange("p t (c i) -> p c t i", i=2)
            split = VECTOR_PAIRS[k]
            if split > 0:
                nc.vector.tensor_copy(out=dst[:, 0:split, :, :], in_=src[:, 0:split, :, :])
            if split < 2 * P:
                nc.scalar.copy(out=dst[:, split : 2 * P, :, :], in_=src[:, split : 2 * P, :, :])

        def quantize_y(k, first=0, count=PACK):
            h, b = divmod(k, BLOCKS)
            lo, hi = first * P, (first + count) * P
            nc.vector.quantize_mx(
                out=y_codes[k][:, lo:hi].bitcast(E4M3X4),
                scales=y_scales[4 * h : P, b * GROUP + lo : b * GROUP + hi],
                in_=y_bf[k % 2][:, PACK * lo : PACK * hi],
            )

        def store_y(k, tiles):
            h, b = divmod(k, BLOCKS)
            dst = out_0[span(b), span(h)].rearrange("(j p) c -> p j c", p=P)
            nc.sync.dma_start(out=dst[:, tiles, :], in_=y_rows[k][:, tiles, :])

        def store_codes(k, first=0, count=PACK):
            h, b = divmod(k, BLOCKS)
            lo, hi = first * P, (first + count) * P
            dst = out_1[h].rearrange("p n t -> p (n t)")[:, PACK * (b * GROUP + lo) : PACK * (b * GROUP + hi)]
            nc.sync.dma_start(out=dst.bitcast(I32), in_=y_codes[k][:, lo:hi].bitcast(I32))

        last = UNITS - 1

        def spread(i):
            words = vec_cols[:, i, 1, :].bitcast(F32)
            for u in range(2):
                nc.tensor.transpose(tr_bank[i][:, span(u, P)], words[:, u : u + 1].to_broadcast([P, P]), ident[:])
            nc.scalar.copy(
                out=vec_rows[:, i, :].bitcast(F32).rearrange("p (m u) -> p m u", u=2),
                in_=tr_bank[i][:, 0 : 2 * P].rearrange("p (u m) -> p m u", u=2),
            )

        def leak_rows(j):
            nc.vector.tensor_tensor(out=held_rows[:, j, :], in0=prev_rows[last][:, j, :], in1=vec_rows[:, 0, :], op=MULT)

        def hold_rows(j):
            nc.vector.tensor_tensor(out=held_rows[:, j, :], in0=held_rows[:, j, :], in1=gain_ref_row[:], op=ADD)

        def mx_rows(j):
            for g in range(PASSES):
                nc.tensor.matmul_mx(
                    out=mx_bank[j][:],
                    lhsT=e_words(g, BLOCKS - 1)[:, span(j, P)].bitcast(E5M2X4),
                    lhsT_scale=e_scales[BLOCKS - 1][:, span(PACK * g + j, P)],
                    rhs=r_codes[1, g][:].bitcast(E4M3X4),
                    rhs_scale=r_scales[1, g][:],
                    start=(g == 0),
                    stop=(g == PASSES - 1),
                )

        def scale_rows(j):
            for half in range(2):
                ms = span(half, P // 2)
                nc.vector.tensor_tensor(
                    out=scaled[j % 2][:].rearrange("p (m t) -> p m t", t=PACK)[:, ms, :],
                    in0=mx_bank[j][:].rearrange("p (t m) -> p m t", t=PACK)[:, ms, :],
                    in1=vec_rows[:, 1, :].rearrange("p (m t) -> p m t", t=PACK)[:, ms, :],
                    op=MULT,
                )

        def add_rows(j):
            for half in range(2):
                cols = span(half, 2 * P)
                nc.vector.tensor_tensor(
                    out=y_rows[last][:, j, cols], in0=held_rows[:, j, cols], in1=scaled[j % 2][:, cols], op=SUBTRACT
                )

        def by_pair(ap):
            return ap.rearrange("p (m u e) -> p u m e", u=2, e=2)

        def round_rows(j):
            nc.scalar.copy(
                out=y_pairs[j][:].rearrange("p (u m e) -> p u m e", u=2, e=2), in_=by_pair(y_rows[last][:, j, :])
            )

        def add_rows_rounded(j):
            for u in range(2):
                nc.vector.tensor_tensor(
                    out=y_pairs[j][:].rearrange("p (u m e) -> p u m e", u=2, e=2)[:, u, :, :],
                    in0=by_pair(held_rows[:, j, :])[:, u, :, :],
                    in1=by_pair(scaled[j % 2][:])[:, u, :, :],
                    op=SUBTRACT,
                )

        def turn_pairs(bank, first, count):
            for j in range(count):
                for u in range(2):
                    words = y_pairs[first + j][:].bitcast(F32)
                    nc.tensor.transpose(bank[:, span(2 * j + u, P)], words[:, span(u, P)], ident[:])

        def copy_pairs(bank, first, count):
            words = y_bf[last % 2][:].bitcast(F32)[:, 2 * P * first : 2 * P * (first + count)]
            nc.scalar.copy(
                out=words.rearrange("p (j r u) -> p j r u", j=count, u=2),
                in_=bank[:, 0 : 2 * P * count].rearrange("p (j u r) -> p j r u", j=count, u=2),
            )

        make_identity(nc, ident[:])
        nc.vector.memset(vec_raw[:].bitcast(U32), 0)
        for b in range(BLOCKS):
            nc.vector.memset(e_scales[b][:].bitcast(U32), 0)

        load_recon(0, 0)
        for i, vec in enumerate((leak, gain, mode_ref)):
            nc.scalar.dma_start(out=vec_raw[2 * i : 2 * i + 2, :], in_=vec.rearrange("(h c) -> h c", h=HALVES))
        load_recon(0, 1)
        load_scales(0)
        load_first_words(0)
        load_recon(0, 2)
        load_first_words(1)
        load_prev(0)
        load_recon(0, 3)
        load_first_words(2)
        load_first_words(3)
        load_prev(1)
        load_scales(1)
        load_word_pair(0, 1)
        load_word_pair(1, 1)

        for g in range(PASSES):
            if g == 1:
                for u in range(2):
                    nc.tensor.transpose(tr_bank[3][:, span(u, P)], vec_raw[:].bitcast(F32)[:, u : 2 * P : 2], ident[:])
                nc.vector.tensor_copy(
                    out=vec_cols[:].bitcast(F32).rearrange("p i h u -> p (i h) u"),
                    in_=tr_bank[3][:, 0 : 2 * P].rearrange("p (u r) -> p r u", u=2)[:, 0 : 3 * HALVES, :],
                )
            if g == 2:
                for i in range(3):
                    spread(i)
                nc.vector.tensor_copy(out=leak_f[:], in_=leak_bf)
                nc.vector.tensor_scalar(out=neg_gain[:], in0=gain_bf, scalar1=-1.0, scalar2=None, op0=MULT)
                nc.vector.tensor_tensor(out=gain_ref[:], in0=gain_bf, in1=ref_bf, op=MULT)
            if g == 3:
                nc.vector.tensor_tensor(out=gain_ref_row[:], in0=vec_rows[:, 1, :], in1=vec_rows[:, 2, :], op=MULT)
            sort_recon(0, g, 0)
            sort_recon(0, g, 1)
            if g > 0:
                quantize_recon(0, g - 1, 1)
            quantize_recon(0, g, 0)
        quantize_recon(0, PASSES - 1, 1)

        load_recon(1, 0)
        load_prev(2)
        load_recon(1, 1)
        load_scales(2)
        load_word_pair(0, 2)
        load_word_pair(1, 2)
        load_prev(3)
        load_recon(1, 2)
        load_recon(1, 3)
        load_prev(4)
        load_prev(last)

        for g in range(PASSES):
            if g == 2:
                turn_prev(0)
                for t in range(PACK):
                    hold_term(0, t)
            for t in range(PACK):
                mx_pass(0, t, g)
        for t in range(PACK):
            update(0, t)
        turn_prev(1)

        def sort_late(g, s):
            if 0 <= g < PASSES:
                sort_recon(1, g, s)

        def quantize_late(g, s):
            if 0 <= g < PASSES:
                quantize_recon(1, g, s)

        for k in range(1, last):
            early, late = 2 * k - 3, 2 * k - 2
            rows = (2 * k - 6, 2 * k - 5) if k >= 3 else ()
            for t in range(PACK):
                hold_term(k, t)
            sort_late(early, 0)
            sort_late(early, 1)
            quantize_late(early - 1, 1)
            quantize_late(early, 0)
            round_y(k - 1)
            for j in rows:
                leak_rows(j)
            for g in range(PASSES):
                for t in (0, 1):
                    mx_pass(k, t, g)
            sort_late(late, 0)
            if not rows:
                quantize_y(k - 1)
            update(k, 0)
            quantize_late(late - 1, 1)
            quantize_late(late, 0)
            update(k, 1)
            for j in rows:
                hold_rows(j)
            for j in range(PACK):
                for t in range(PACK):
                    turn_y(k - 1, j, t)
                copy_y(k - 1, j)
                store_y(k - 1, slice(j, j + 1))
            sort_late(late, 1)
            for t in (2, 3):
                for g in range(PASSES):
                    mx_pass(k, t, g)
                update(k, t)
                if rows and t == 2:
                    quantize_y(k - 1)
            store_codes(k - 1)
            if k + 1 < last:
                turn_prev(k + 1)

        k = last - 1
        mx_rows(0)
        for t in range(PACK):
            for j in range(PACK):
                turn_y(k, j, t)
        scale_rows(0)
        add_rows(0)
        round_y(k)
        quantize_y(k)
        store_y(last, slice(0, 1))
        for j in range(PACK):
            copy_y(k, j)
            store_y(k, slice(j, j + 1))
        store_codes(k)
        round_rows(0)
        for j in (1, 2):
            mx_rows(j)
            scale_rows(j)
            add_rows(j)
            round_rows(j)
            store_y(last, slice(j, j + 1))
        mx_rows(3)
        scale_rows(3)
        add_rows_rounded(3)
        add_rows(3)
        parts = ((0, 2), (2, 1), (3, 1))
        for i, (first, count) in enumerate(parts):
            turn_pairs(tr_bank[i], first, count)
            copy_pairs(tr_bank[i], first, count)
            quantize_y(last, first, count)
        store_y(last, slice(3, 4))
        store_codes(last, 0, 2)
        store_codes(last, 2, 2)
        for q in range(4):
            queue = nc.scalar if q < 3 else nc.sync
            queue.dma_start(
                out=out_2[:, 4 * q : 4 * q + 4, :].bitcast(I32), in_=y_scales[32 * q : 32 * q + 8, :].bitcast(I32)
            )
